import numpy as np
import ml_dtypes


def mxq(x, axis, fmt="e4m3"):
    dtype, down = {"e4m3": (ml_dtypes.float8_e4m3fn, 7), "e5m2": (ml_dtypes.float8_e5m2, 14)}[fmt]
    v = np.moveaxis(np.asarray(x, np.float32).astype(ml_dtypes.bfloat16).astype(np.float64), axis, -1)
    blocks = v.reshape(v.shape[:-1] + (-1, 32))
    amax = np.abs(blocks).max(-1, keepdims=True)
    byte = np.maximum(np.where(amax > 0, np.frexp(amax)[1] - 1 + 127, 0) - down, 1)
    scale = np.exp2(byte - 127.0)
    codes = (blocks / scale).astype(np.float32).astype(dtype).astype(np.float64)
    return np.moveaxis((codes * scale).reshape(v.shape), -1, axis)


WIDE = False


def mx_kscale(k):
    if not WIDE:
        return np.ones(k)
    levels = np.array([10, -10, 5, -5, 0])
    if k % 512:
        return np.exp2(np.random.permutation(np.resize(levels, k // 32))).repeat(32)
    a = np.empty((k // 512, 16))
    for p in range(k // 512):
        a[p, :8] = np.random.permutation(np.resize(levels, 8))
        for g in range(8):
            far = levels[np.abs(levels - a[p, g]) >= 10]
            a[p, g + 8] = far[np.random.randint(len(far))]
    return np.exp2(a.ravel()).repeat(32)


def f64(x):
    return np.asarray(x).astype(np.float64)


def striped(idx):
    return np.tile(idx.reshape(-1, 16).T, (8, 1)).astype(np.uint16)


def unstriped(offs):
    return offs[:16].T.reshape(-1).astype(np.int64)


def pack_weight(w):
    k, n = w.shape
    w = f64(np.asarray(w, np.float32).astype(ml_dtypes.bfloat16)).reshape(k // 32, 32, n)
    amax = np.abs(w).max(1)
    byte = np.clip(np.where(amax > 0, np.frexp(amax)[1] - 1 + 127 - 7, 1), 1, 254)
    scaled = (w * np.exp2(127.0 - byte)[:, None, :]).reshape(k, n).astype(np.float32)
    words = np.ascontiguousarray(scaled.reshape(k // 512, 128, 4, n).transpose(0, 1, 3, 2)).astype(ml_dtypes.float8_e4m3fn).view(np.uint8)
    return words, np.ascontiguousarray(byte.astype(np.uint8).reshape(k // 512, 16, n))


def unpack_weight(words, scales):
    g, p, n, _ = words.shape
    vals = np.ascontiguousarray(words).view(ml_dtypes.float8_e4m3fn).astype(np.float64) * np.repeat(np.exp2(scales.astype(np.float64) - 127.0), 8, axis=1)[..., None]
    return vals.transpose(0, 1, 3, 2).reshape(g * 512, n)


K, T, S, H, V, Z, W = 512, 1024, 512, 512, 256, 512, 2048
P = 2 ** 7


def setup_inputs():
    n = np.random.standard_normal
    s = mx_kscale(K)[:, None]
    packed_xT = pack_weight(n((K, T)) * s)
    packed_eT = pack_weight(n((K, W)) * s)
    return {
        "x_words": packed_xT[0],
        "x_scales": packed_xT[1],
        "w1": (n((K, H)) / np.sqrt(K) / s).astype(np.float32),
        "e_words": packed_eT[0],
        "e_scales": packed_eT[1],
        "exq": (n((H, V))).astype(np.float32),
        "unit": (np.random.uniform(0.6, 1.4, (K, 1)) / np.sqrt(K) / s).astype(np.float32),
        "wgt": (np.tile(np.random.uniform(0.2, 1.4, W), (P, 1))).astype(np.float32),
        "offs": striped(np.random.permutation(T)[:S]),
        "bm1": striped(np.random.permutation(S)),
        "bm2": striped(np.random.permutation(S)),
        "ps": striped(np.random.permutation(S)[:V]),
        "prt": striped(np.random.permutation(W)[:Z]),
        "anc": striped(np.random.permutation(Z)),
    }


def reference(x_words, x_scales, w1, e_words, e_scales, exq, unit, wgt, offs, bm1, bm2, ps, prt, anc):
    xq = unpack_weight(x_words, x_scales)[:, unstriped(offs)]
    y = mxq(f64(w1), 0, "e4m3").T @ xq
    y1 = y[:, unstriped(bm1)]
    y2 = y[:, unstriped(bm2)]
    rng_ = np.minimum(y, y1) + np.maximum(y, y2)
    inn = rng_[:, unstriped(ps)] - f64(exq)
    hid = f64(unit) * inn
    e_prt = unpack_weight(e_words, e_scales)[:, unstriped(prt)]
    sc = mxq(hid, 0, "e4m3").T @ e_prt
    ll = -2.0 * ((np.tanh(sc)) ** 2)
    pw_ = np.exp(ll) * (f64(wgt)[:1][:, unstriped(prt)])
    tot = pw_.mean(axis=1, keepdims=True)
    nw = pw_ / (tot + 0.1)
    lnw = np.log(nw + 0.2)
    return lnw * (f64(wgt)[:1][:, unstriped(prt)]) - nw[:, unstriped(anc)]

@@ -1,0 +1,178 @@
+from contextlib import ExitStack
+
+import concourse.mybir as mybir
+
+K, T, S, H, V, Z, W = 512, 1024, 512, 512, 256, 512, 2048
+FLOPS = 2 * K * H * S + 2 * H * V * Z
+
+F32 = mybir.dt.float32
+BF16 = mybir.dt.bfloat16
+I32 = mybir.dt.int32
+U32 = mybir.dt.uint32
+U16 = mybir.dt.uint16
+U8 = mybir.dt.uint8
+FP8X4 = mybir.dt.float8_e4m3fn_x4
+ALU = mybir.AluOpType
+ACT = mybir.ActivationFunctionType
+
+P = 128
+PACK = 4
+PAD = 8
+
+
+def tile_picked_ymaprel_log_p_kernel(
+    tc, x_words, x_scales, w1, e_words, e_scales, exq, unit, wgt, offs, bm1, bm2, ps, prt, anc, out
+):
+    nc = tc.nc
+    with ExitStack() as ctx:
+        keep = ctx.enter_context(tc.tile_pool(name="keep", bufs=1))
+        psum = ctx.enter_context(tc.psum_pool(name="psum", bufs=1))
+
+        def sb(name, shape, dtype):
+            return keep.tile(shape, dtype, name=name, align_bytes=64)
+
+        def load_list(name, src):
+            lst = sb(name, list(src.shape), U16)
+            nc.sync.dma_start(lst[:], src)
+            return lst
+
+        def load_scales(queue, plane, src):
+            for q in range(4):
+                queue.dma_start(plane[32 * q : 32 * q + 4, :].bitcast(I32), src[0, 4 * q : 4 * q + 4, :].bitcast(I32))
+
+        def load_words(name, src, width):
+            words = sb(name, [P, width], I32)
+            nc.sync.dma_start(words[:], src[0].rearrange("p n t -> p (n t)").bitcast(I32))
+            return words
+
+        xs_all = sb("xs_all", [P, T], U8)
+        es_all = sb("es_all", [P, W], U8)
+        nc.vector.memset(xs_all[:].bitcast(I32), 0)
+        nc.vector.memset(es_all[:].bitcast(I32), 0)
+        y_sb = [sb(f"y{t}", [P, S + PAD], F32) for t in range(PACK)]
+        for t in range(PACK):
+            nc.vector.memset(y_sb[t][:, S:], 0.0)
+
+        offs_l = load_list("offs_l", offs)
+        load_scales(nc.scalar, xs_all, x_scales)
+        w_view = w1.rearrange("(p j) c -> p j c", j=PACK)
+        w_raw = [sb(f"w_raw{h}", [P, PACK, H // 2], F32) for h in range(2)]
+        nc.sync.dma_start(w_raw[0][:], w_view[:, :, : H // 2])
+        xw_all = load_words("xw_all", x_words, T)
+        nc.sync.dma_start(w_raw[1][:], w_view[:, :, H // 2 :])
+        bm1_l = load_list("bm1_l", bm1)
+        bm2_l = load_list("bm2_l", bm2)
+        prt_l = load_list("prt_l", prt)
+        load_scales(nc.sync, es_all, e_scales)
+        ew_all = load_words("ew_all", e_words, W)
+        unit_sb = sb("unit_sb", [P, PACK], F32)
+        nc.sync.dma_start(unit_sb[:], unit.rearrange("(p t) o -> p (t o)", t=PACK))
+        ps_l = load_list("ps_l", ps)
+        exq_sb = sb("exq_sb", [P, PACK, V], F32)
+        nc.sync.dma_start(exq_sb[:], exq.rearrange("(p t) v -> p t v", t=PACK))
+        wgt_all = sb("wgt_all", [P, W], F32)
+        nc.sync.dma_start(wgt_all[:], wgt)
+        anc_l = load_list("anc_l", anc)
+
+        xs = sb("xs", [P, S], U8)
+        xw = sb("xw", [P, S], U32)
+        w_bf = sb("w_bf", [P, PACK, P, PACK], BF16)
+        w_codes = sb("w_codes", [P, H], U32)
+        w_sc = sb("w_sc", [P, H], U8)
+        nc.vector.tensor_copy(xs[:], xs_all[:].indirect(offs_l[:]))
+        nc.scalar.copy(
+            w_bf[:, :, : P // 2, :].rearrange("p t m j -> p m j t"),
+            w_raw[0][:].rearrange("p j (m t) -> p m j t", t=PACK),
+        )
+        nc.vector.tensor_copy(xw[:], xw_all[:].bitcast(U32).indirect(offs_l[:]))
+        nc.vector.tensor_copy(
+            w_bf[:, :, P // 2 :, :].rearrange("p t m j -> p m j t"),
+            w_raw[1][:].rearrange("p j (m t) -> p m j t", t=PACK),
+        )
+        y_ps = [psum.tile([P, S], F32, name=f"y_ps{t}") for t in range(PACK)]
+        for t in range(PACK):
+            cols = slice(t * P, (t + 1) * P)
+            nc.vector.quantize_mx(
+                out=w_codes[:, cols].bitcast(FP8X4), scales=w_sc[:, cols], in_=w_bf[:, t].rearrange("p m j -> p (m j)")
+            )
+            nc.tensor.matmul_mx(
+                out=y_ps[t][:], lhsT=w_codes[:, cols].bitcast(FP8X4), lhsT_scale=w_sc[:, cols],
+                rhs=xw[:].bitcast(FP8X4), rhs_scale=xs[:], start=True, stop=True,
+            )
+
+        es = sb("es", [P, Z], U8)
+        ew = sb("ew", [P, Z], U32)
+        wg = sb("wg", [P, Z], F32)
+        nc.vector.tensor_copy(es[:], es_all[:].indirect(prt_l[:]))
+        nc.vector.tensor_copy(ew[:], ew_all[:].bitcast(U32).indirect(prt_l[:]))
+
+        exu = sb("exu", [P, PACK, V], F32)
+        for t in range(PACK):
+            nc.gpsimd.tensor_scalar(exu[:, t, :], exq_sb[:, t, :], unit_sb[:, t : t + 1], 0.0, ALU.mult, ALU.add)
+
+        hid = sb("hid", [P, PACK, V], F32)
+        for t in range(PACK):
+            y1 = sb(f"y1_{t}", [P, S], F32)
+            y2 = sb(f"y2_{t}", [P, S], F32)
+            rng = sb(f"rng{t}", [P, S], F32)
+            picked = sb(f"picked{t}", [P, V], F32)
+            nc.scalar.copy(y_sb[t][:, :S], y_ps[t][:])
+            nc.scalar.activation(y1[:], y_sb[t][:].indirect(bm1_l[:]), ACT.Copy)
+            nc.scalar.activation(y2[:], y_sb[t][:].indirect(bm2_l[:]), ACT.Copy)
+            nc.vector.tensor_tensor(y1[:], y_ps[t][:], y1[:], ALU.min)
+            nc.vector.tensor_tensor(y2[:], y_ps[t][:], y2[:], ALU.max)
+            nc.vector.tensor_tensor(rng[:], y1[:], y2[:], ALU.add)
+            nc.vector.tensor_copy(picked[:], rng[:].indirect(ps_l[:]))
+            nc.vector.scalar_tensor_tensor(
+                hid[:, t, :], picked[:], unit_sb[:, t : t + 1], exu[:, t, :], ALU.mult, ALU.subtract
+            )
+            if t == 0:
+                nc.vector.tensor_copy(wg[:], wgt_all[:].indirect(prt_l[:]))
+
+        h_codes = sb("h_codes", [P, V], U32)
+        h_sc = sb("h_sc", [P, V], U8)
+        sc_ps = [psum.tile([P, Z], F32, name=f"sc_ps{h}") for h in range(2)]
+        for h in range(2):
+            cols = slice(h * P, (h + 1) * P)
+            h_bf = sb(f"h_bf{h}", [P, P, PACK], BF16)
+            nc.vector.tensor_copy(
+                h_bf[:].rearrange("p (c i) t -> p c t i", i=4),
+                hid[:, :, cols].rearrange("p t (c i) -> p c t i", i=4),
+            )
+            nc.vector.quantize_mx(
+                out=h_codes[:, cols].bitcast(FP8X4), scales=h_sc[:, cols], in_=h_bf[:].rearrange("p v t -> p (v t)")
+            )
+            nc.tensor.matmul_mx(
+                out=sc_ps[h][:], lhsT=h_codes[:, cols].bitcast(FP8X4), lhsT_scale=h_sc[:, cols],
+                rhs=ew[:].bitcast(FP8X4), rhs_scale=es[:], start=True, stop=True,
+            )
+
+        th = [sb(f"th{h}", [P, Z], F32) for h in range(2)]
+        sq = [sb(f"sq{h}", [P, Z], F32) for h in range(2)]
+        ex = [sb(f"ex{h}", [P, Z], F32) for h in range(2)]
+        pw = [sb(f"pw{h}", [P, Z], F32) for h in range(2)]
+        pa = [sb(f"pa{h}", [P, Z], F32) for h in range(2)]
+        ln = [sb(f"ln{h}", [P, Z], F32) for h in range(2)]
+        res = [sb(f"res{h}", [P, Z], F32) for h in range(2)]
+        st = [sb(f"st{h}", [P, 4], F32) for h in range(2)]
+        for h in range(2):
+            nc.scalar.activation(th[h][:], sc_ps[h][:], ACT.Tanh)
+            if h == 0:
+                nc.scalar.activation(sq[h][:], th[h][:], ACT.Square)
+            else:
+                nc.vector.tensor_tensor(sq[h][:], th[h][:], th[h][:], ALU.mult)
+        for h in range(2):
+            nc.scalar.activation(ex[h][:], sq[h][:], ACT.Exp, scale=-2.0)
+            nc.vector.scalar_tensor_tensor(pw[h][:], ex[h][:], 1.0, wg[:], ALU.mult, ALU.mult, accum_out=st[h][:, 0:1])
+            nc.vector.tensor_scalar(st[h][:, 1:2], st[h][:, 0:1], 1.0 / Z, 0.1, ALU.mult, ALU.add)
+            nc.vector.reciprocal(st[h][:, 2:3], st[h][:, 1:2])
+            nc.vector.tensor_scalar(st[h][:, 3:4], st[h][:, 2:3], -1.0, None, ALU.mult)
+            for c in range(2):
+                nc.vector.tensor_copy(
+                    pa[h][:, c * 256 : (c + 1) * 256], pw[h][:].indirect(anc_l[:, c * 16 : (c + 1) * 16])
+                )
+        for h in range(2):
+            nc.scalar.activation(ln[h][:], pw[h][:], ACT.Ln, bias=0.2, scale=st[h][:, 2:3])
+            nc.vector.tensor_tensor(ln[h][:], ln[h][:], wg[:], ALU.mult)
+            nc.vector.scalar_tensor_tensor(res[h][:], pa[h][:], st[h][:, 3:4], ln[h][:], ALU.mult, ALU.add)
+            nc.sync.dma_start(out[h * P : (h + 1) * P, :], res[h][:])

@@ -47,29 +47,29 @@ def tile_picked_ymaprel_log_p_kernel(
 
         xs_all = sb("xs_all", [P, T], U8)
         es_all = sb("es_all", [P, W], U8)
-        nc.vector.memset(xs_all[:].bitcast(I32), 0)
+        nc.gpsimd.memset(xs_all[:].bitcast(I32), 0)
         nc.vector.memset(es_all[:].bitcast(I32), 0)
         y_sb = [sb(f"y{t}", [P, S + PAD], F32) for t in range(PACK)]
         for t in range(PACK):
             nc.vector.memset(y_sb[t][:, S:], 0.0)
 
         offs_l = load_list("offs_l", offs)
-        load_scales(nc.scalar, xs_all, x_scales)
         w_view = w1.rearrange("(p j) c -> p j c", j=PACK)
         w_raw = [sb(f"w_raw{h}", [P, PACK, H // 2], F32) for h in range(2)]
         nc.sync.dma_start(w_raw[0][:], w_view[:, :, : H // 2])
+        load_scales(nc.sync, xs_all, x_scales)
         xw_all = load_words("xw_all", x_words, T)
         nc.sync.dma_start(w_raw[1][:], w_view[:, :, H // 2 :])
+        prt_l = load_list("prt_l", prt)
         bm1_l = load_list("bm1_l", bm1)
         bm2_l = load_list("bm2_l", bm2)
-        prt_l = load_list("prt_l", prt)
         load_scales(nc.sync, es_all, e_scales)
-        ew_all = load_words("ew_all", e_words, W)
         unit_sb = sb("unit_sb", [P, PACK], F32)
         nc.sync.dma_start(unit_sb[:], unit.rearrange("(p t) o -> p (t o)", t=PACK))
-        ps_l = load_list("ps_l", ps)
         exq_sb = sb("exq_sb", [P, PACK, V], F32)
         nc.sync.dma_start(exq_sb[:], exq.rearrange("(p t) v -> p t v", t=PACK))
+        ps_l = load_list("ps_l", ps)
+        ew_all = load_words("ew_all", e_words, W)
         wgt_all = sb("wgt_all", [P, W], F32)
         nc.sync.dma_start(wgt_all[:], wgt)
         anc_l = load_list("anc_l", anc)
@@ -85,9 +85,14 @@ def tile_picked_ymaprel_log_p_kernel(
             w_raw[0][:].rearrange("p j (m t) -> p m j t", t=PACK),
         )
         nc.vector.tensor_copy(xw[:], xw_all[:].bitcast(U32).indirect(offs_l[:]))
+        M_SPLIT = 24
+        nc.scalar.copy(
+            w_bf[:, :, P // 2 : P // 2 + M_SPLIT, :].rearrange("p t m j -> p m j t"),
+            w_raw[1][:, :, : M_SPLIT * PACK].rearrange("p j (m t) -> p m j t", t=PACK),
+        )
         nc.vector.tensor_copy(
-            w_bf[:, :, P // 2 :, :].rearrange("p t m j -> p m j t"),
-            w_raw[1][:].rearrange("p j (m t) -> p m j t", t=PACK),
+            w_bf[:, :, P // 2 + M_SPLIT :, :].rearrange("p t m j -> p m j t"),
+            w_raw[1][:, :, M_SPLIT * PACK :].rearrange("p j (m t) -> p m j t", t=PACK),
         )
         y_ps = [psum.tile([P, S], F32, name=f"y_ps{t}") for t in range(PACK)]
         for t in range(PACK):
@@ -101,78 +106,128 @@ def tile_picked_ymaprel_log_p_kernel(
             )
 
         es = sb("es", [P, Z], U8)
-        ew = sb("ew", [P, Z], U32)
-        wg = sb("wg", [P, Z], F32)
         nc.vector.tensor_copy(es[:], es_all[:].indirect(prt_l[:]))
-        nc.vector.tensor_copy(ew[:], ew_all[:].bitcast(U32).indirect(prt_l[:]))
 
-        exu = sb("exu", [P, PACK, V], F32)
-        for t in range(PACK):
-            nc.gpsimd.tensor_scalar(exu[:, t, :], exq_sb[:, t, :], unit_sb[:, t : t + 1], 0.0, ALU.mult, ALU.add)
-
-        hid = sb("hid", [P, PACK, V], F32)
-        for t in range(PACK):
-            y1 = sb(f"y1_{t}", [P, S], F32)
-            y2 = sb(f"y2_{t}", [P, S], F32)
-            rng = sb(f"rng{t}", [P, S], F32)
-            picked = sb(f"picked{t}", [P, V], F32)
-            nc.scalar.copy(y_sb[t][:, :S], y_ps[t][:])
-            nc.scalar.activation(y1[:], y_sb[t][:].indirect(bm1_l[:]), ACT.Copy)
-            nc.scalar.activation(y2[:], y_sb[t][:].indirect(bm2_l[:]), ACT.Copy)
-            nc.vector.tensor_tensor(y1[:], y_ps[t][:], y1[:], ALU.min)
-            nc.vector.tensor_tensor(y2[:], y_ps[t][:], y2[:], ALU.max)
-            nc.vector.tensor_tensor(rng[:], y1[:], y2[:], ALU.add)
-            nc.vector.tensor_copy(picked[:], rng[:].indirect(ps_l[:]))
-            nc.vector.scalar_tensor_tensor(
-                hid[:, t, :], picked[:], unit_sb[:, t : t + 1], exu[:, t, :], ALU.mult, ALU.subtract
+        last = PACK - 1
+        ON_GPSIMD = 2
+        exu = sb("exu", [P, PACK - ON_GPSIMD, V], F32)
+        for t in range(ON_GPSIMD, PACK):
+            nc.gpsimd.tensor_scalar(
+                exu[:, t - ON_GPSIMD, :], exq_sb[:, t, :], unit_sb[:, t : t + 1], 0.0, ALU.mult, ALU.add
             )
-            if t == 0:
-                nc.vector.tensor_copy(wg[:], wgt_all[:].indirect(prt_l[:]))
+
+        hid_flat = sb("hid_flat", [P, PACK * V], F32)
+        hid = hid_flat[:].rearrange("p (t v) -> p t v", t=PACK)
+        rng = [sb(f"rng{t}", [P, S], F32) for t in range(PACK)]
+        y1 = [sb(f"y1_{t}", [P, S], F32)[:] for t in range(last)] + [hid_flat[:, ON_GPSIMD * V :]]
+        y2 = [sb(f"y2_{t}", [P, S], F32) for t in range(last)] + [rng[1]]
+        picked = [sb(f"picked{t}", [P, V], F32)[:] if t != 2 else y_sb[last][:, :V] for t in range(PACK)]
+        halves = [(0, S // 2), (S // 2, S)]
+
+        def gather(on_vector, dst, window, lst, a, b):
+            src = window[:].indirect(lst[:, a // 16 : b // 16])
+            if on_vector:
+                nc.vector.tensor_copy(dst[:, a:b], src)
+            else:
+                nc.scalar.activation(dst[:, a:b], src, ACT.Copy)
+
+        def innovate(t, a, b):
+            nc.vector.scalar_tensor_tensor(
+                hid[:, t, a:b], picked[t][:, a:b], unit_sb[:, t : t + 1], exu[:, t - ON_GPSIMD, a:b], ALU.mult, ALU.subtract
+            )
+
+        def pick(t):
+            gather(False, picked[t], rng[t], ps_l, 0, V)
+            if t < ON_GPSIMD:
+                nc.gpsimd.tensor_tensor(picked[t], picked[t], exq_sb[:, t, :], ALU.subtract)
+                nc.gpsimd.tensor_scalar(hid[:, t, :], picked[t], unit_sb[:, t : t + 1], 0.0, ALU.mult, ALU.add)
+
+        for t in range(last):
+            nc.scalar.copy(y_sb[t][:, :S], y_ps[t][:])
+            gather(False, y1[t], y_sb[t], bm1_l, 0, S)
+            for a, b in halves:
+                gather(t < last - 1 or a == 0, y2[t], y_sb[t], bm2_l, a, b)
+            nc.vector.tensor_tensor(y1[t], y_ps[t][:], y1[t], ALU.min)
+            nc.vector.tensor_tensor(y2[t][:], y_ps[t][:], y2[t][:], ALU.max)
+            nc.gpsimd.tensor_tensor(rng[t][:], y1[t], y2[t][:], ALU.add)
+        ew = keep.tile([P, Z], U32, name="ew", tag="y2", align_bytes=64)
+        nc.vector.tensor_copy(ew[:], ew_all[:].bitcast(U32).indirect(prt_l[:]))
+        nc.scalar.copy(y_sb[last][:, :S], y_ps[last][:])
+        pick(0)
+        gather(False, y1[last], y_sb[last], bm1_l, 0, S)
+        nc.vector.tensor_tensor(y1[last], y_ps[last][:], y1[last], ALU.min)
+        pick(1)
+        for a, b in halves:
+            gather(False, y2[last], y_sb[last], bm2_l, a, b)
+            nc.vector.tensor_tensor(y2[last][:, a:b], y_ps[last][:, a:b], y2[last][:, a:b], ALU.max)
+        nc.vector.tensor_tensor(rng[last][:], y1[last], y2[last][:], ALU.add)
+        pick(2)
+        for h in range(2):
+            gather(h == 0, picked[last], rng[last], ps_l, h * P, (h + 1) * P)
+        innovate(2, 0, V)
+        for h in range(2):
+            innovate(last, h * P, (h + 1) * P)
 
         h_codes = sb("h_codes", [P, V], U32)
         h_sc = sb("h_sc", [P, V], U8)
-        sc_ps = [psum.tile([P, Z], F32, name=f"sc_ps{h}") for h in range(2)]
+        sc_ps = [[psum.tile([P, Z // 2], F32, name=f"sc_ps{h}{c}") for c in range(2)] for h in range(2)]
         for h in range(2):
             cols = slice(h * P, (h + 1) * P)
             h_bf = sb(f"h_bf{h}", [P, P, PACK], BF16)
-            nc.vector.tensor_copy(
+            (nc.vector.tensor_copy if h == 0 else nc.scalar.copy)(
                 h_bf[:].rearrange("p (c i) t -> p c t i", i=4),
                 hid[:, :, cols].rearrange("p t (c i) -> p c t i", i=4),
             )
             nc.vector.quantize_mx(
                 out=h_codes[:, cols].bitcast(FP8X4), scales=h_sc[:, cols], in_=h_bf[:].rearrange("p v t -> p (v t)")
             )
-            nc.tensor.matmul_mx(
-                out=sc_ps[h][:], lhsT=h_codes[:, cols].bitcast(FP8X4), lhsT_scale=h_sc[:, cols],
-                rhs=ew[:].bitcast(FP8X4), rhs_scale=es[:], start=True, stop=True,
-            )
+            for c, (a, b) in enumerate(halves):
+                nc.tensor.matmul_mx(
+                    out=sc_ps[h][c][:], lhsT=h_codes[:, cols].bitcast(FP8X4), lhsT_scale=h_sc[:, cols],
+                    rhs=ew[:, a:b].bitcast(FP8X4), rhs_scale=es[:, a:b], start=True, stop=True,
+                )
 
+        wg_tile = keep.tile([P, Z], F32, name="wg_tile", tag="hid_flat", align_bytes=64)
+        wg = wg_tile[:]
+        gather(True, wg, wgt_all, prt_l, 0, Z)
         th = [sb(f"th{h}", [P, Z], F32) for h in range(2)]
         sq = [sb(f"sq{h}", [P, Z], F32) for h in range(2)]
         ex = [sb(f"ex{h}", [P, Z], F32) for h in range(2)]
         pw = [sb(f"pw{h}", [P, Z], F32) for h in range(2)]
-        pa = [sb(f"pa{h}", [P, Z], F32) for h in range(2)]
+        pa = [sb(f"pa{h}", [P, Z + PAD], F32) for h in range(2)]
         ln = [sb(f"ln{h}", [P, Z], F32) for h in range(2)]
         res = [sb(f"res{h}", [P, Z], F32) for h in range(2)]
         st = [sb(f"st{h}", [P, 4], F32) for h in range(2)]
+        inv_col = [Z // 2, 0]
+        inv = [pa[1][:, c : c + 1] for c in inv_col]
+        neg_inv = [pa[1][:, Z + h : Z + h + 1] for h in range(2)]
+        signs = sb("signs", [P, 2], F32)
+        nc.vector.memset(signs[:, 0:1], 1.0 / Z)
+        nc.vector.memset(signs[:, 1:2], -1.0 / Z)
         for h in range(2):
-            nc.scalar.activation(th[h][:], sc_ps[h][:], ACT.Tanh)
-            if h == 0:
-                nc.scalar.activation(sq[h][:], th[h][:], ACT.Square)
-            else:
-                nc.vector.tensor_tensor(sq[h][:], th[h][:], th[h][:], ALU.mult)
+            for c, (a, b) in enumerate(halves):
+                nc.scalar.activation(th[h][:, a:b], sc_ps[h][c][:], ACT.Tanh)
+                nc.vector.tensor_tensor(sq[h][:, a:b], th[h][:, a:b], th[h][:, a:b], ALU.mult)
         for h in range(2):
             nc.scalar.activation(ex[h][:], sq[h][:], ACT.Exp, scale=-2.0)
-            nc.vector.scalar_tensor_tensor(pw[h][:], ex[h][:], 1.0, wg[:], ALU.mult, ALU.mult, accum_out=st[h][:, 0:1])
-            nc.vector.tensor_scalar(st[h][:, 1:2], st[h][:, 0:1], 1.0 / Z, 0.1, ALU.mult, ALU.add)
-            nc.vector.reciprocal(st[h][:, 2:3], st[h][:, 1:2])
-            nc.vector.tensor_scalar(st[h][:, 3:4], st[h][:, 2:3], -1.0, None, ALU.mult)
-            for c in range(2):
-                nc.vector.tensor_copy(
-                    pa[h][:, c * 256 : (c + 1) * 256], pw[h][:].indirect(anc_l[:, c * 16 : (c + 1) * 16])
-                )
+            nc.vector.scalar_tensor_tensor(pw[h][:], ex[h][:], 1.0, wg, ALU.mult, ALU.mult, accum_out=st[h][:, 0:1])
+            nc.vector.scalar_tensor_tensor(
+                st[h][:, 2:4], st[h][:, 0:1].to_broadcast([P, 2]), 0.1 * Z, signs[:], ALU.add, ALU.mult
+            )
+            nc.vector.reciprocal(pa[1][:, inv_col[h] : Z + h + 1 : Z + h - inv_col[h]], st[h][:, 2:4])
+        halves = [slice(0, Z // 2), slice(Z // 2, Z)]
+        for c in range(2):
+            nc.vector.tensor_copy(pa[0][:, halves[c]], pw[0][:].indirect(anc_l[:, c * 16 : (c + 1) * 16]))
         for h in range(2):
-            nc.scalar.activation(ln[h][:], pw[h][:], ACT.Ln, bias=0.2, scale=st[h][:, 2:3])
-            nc.vector.tensor_tensor(ln[h][:], ln[h][:], wg[:], ALU.mult)
-            nc.vector.scalar_tensor_tensor(res[h][:], pa[h][:], st[h][:, 3:4], ln[h][:], ALU.mult, ALU.add)
-            nc.sync.dma_start(out[h * P : (h + 1) * P, :], res[h][:])
+            nc.scalar.activation(ln[h][:], pw[h][:], ACT.Ln, bias=0.2, scale=inv[h])
+        for c in range(2):
+            nc.scalar.activation(pa[1][:, halves[c]], pw[1][:].indirect(anc_l[:, c * 16 : (c + 1) * 16]), ACT.Copy)
+        nc.vector.tensor_tensor(ln[0][:], ln[0][:], wg, ALU.mult)
+        nc.vector.tensor_tensor(ln[1][:], ln[1][:], wg, ALU.mult)
+        nc.vector.scalar_tensor_tensor(res[0][:], pa[0][:, :Z], neg_inv[0], ln[0][:], ALU.mult, ALU.add)
+        nc.sync.dma_start(out[0:P, :], res[0][:])
+        for c in range(2):
+            nc.vector.scalar_tensor_tensor(
+                res[1][:, halves[c]], pa[1][:, halves[c]], neg_inv[1], ln[1][:, halves[c]], ALU.mult, ALU.add
+            )
+            nc.sync.dma_start(out[P : 2 * P, halves[c]], res[1][:, halves[c]])

from contextlib import ExitStack

import concourse.mybir as mybir

K, T, S, H, V, Z, W = 512, 1024, 512, 512, 256, 512, 2048
FLOPS = 2 * K * H * S + 2 * H * V * Z

F32 = mybir.dt.float32
BF16 = mybir.dt.bfloat16
I32 = mybir.dt.int32
U32 = mybir.dt.uint32
U16 = mybir.dt.uint16
U8 = mybir.dt.uint8
FP8X4 = mybir.dt.float8_e4m3fn_x4
ALU = mybir.AluOpType
ACT = mybir.ActivationFunctionType

P = 128
PACK = 4
PAD = 8


def tile_picked_ymaprel_log_p_kernel(
    tc, x_words, x_scales, w1, e_words, e_scales, exq, unit, wgt, offs, bm1, bm2, ps, prt, anc, out
):
    nc = tc.nc
    with ExitStack() as ctx:
        keep = ctx.enter_context(tc.tile_pool(name="keep", bufs=1))
        psum = ctx.enter_context(tc.psum_pool(name="psum", bufs=1))

        def sb(name, shape, dtype):
            return keep.tile(shape, dtype, name=name, align_bytes=64)

        def load_list(name, src):
            lst = sb(name, list(src.shape), U16)
            nc.sync.dma_start(lst[:], src)
            return lst

        def load_scales(queue, plane, src):
            for q in range(4):
                queue.dma_start(plane[32 * q : 32 * q + 4, :].bitcast(I32), src[0, 4 * q : 4 * q + 4, :].bitcast(I32))

        def load_words(name, src, width):
            words = sb(name, [P, width], I32)
            nc.sync.dma_start(words[:], src[0].rearrange("p n t -> p (n t)").bitcast(I32))
            return words

        xs_all = sb("xs_all", [P, T], U8)
        es_all = sb("es_all", [P, W], U8)
        nc.gpsimd.memset(xs_all[:].bitcast(I32), 0)
        nc.vector.memset(es_all[:].bitcast(I32), 0)
        y_sb = [sb(f"y{t}", [P, S + PAD], F32) for t in range(PACK)]
        for t in range(PACK):
            nc.vector.memset(y_sb[t][:, S:], 0.0)

        offs_l = load_list("offs_l", offs)
        w_view = w1.rearrange("(p j) c -> p j c", j=PACK)
        w_raw = [sb(f"w_raw{h}", [P, PACK, H // 2], F32) for h in range(2)]
        nc.sync.dma_start(w_raw[0][:], w_view[:, :, : H // 2])
        load_scales(nc.sync, xs_all, x_scales)
        xw_all = load_words("xw_all", x_words, T)
        nc.sync.dma_start(w_raw[1][:], w_view[:, :, H // 2 :])
        prt_l = load_list("prt_l", prt)
        bm1_l = load_list("bm1_l", bm1)
        bm2_l = load_list("bm2_l", bm2)
        load_scales(nc.sync, es_all, e_scales)
        unit_sb = sb("unit_sb", [P, PACK], F32)
        nc.sync.dma_start(unit_sb[:], unit.rearrange("(p t) o -> p (t o)", t=PACK))
        exq_sb = sb("exq_sb", [P, PACK, V], F32)
        nc.sync.dma_start(exq_sb[:], exq.rearrange("(p t) v -> p t v", t=PACK))
        ps_l = load_list("ps_l", ps)
        ew_all = load_words("ew_all", e_words, W)
        wgt_all = sb("wgt_all", [P, W], F32)
        nc.sync.dma_start(wgt_all[:], wgt)
        anc_l = load_list("anc_l", anc)

        xs = sb("xs", [P, S], U8)
        xw = sb("xw", [P, S], U32)
        w_bf = sb("w_bf", [P, PACK, P, PACK], BF16)
        w_codes = sb("w_codes", [P, H], U32)
        w_sc = sb("w_sc", [P, H], U8)
        nc.vector.tensor_copy(xs[:], xs_all[:].indirect(offs_l[:]))
        nc.scalar.copy(
            w_bf[:, :, : P // 2, :].rearrange("p t m j -> p m j t"),
            w_raw[0][:].rearrange("p j (m t) -> p m j t", t=PACK),
        )
        nc.vector.tensor_copy(xw[:], xw_all[:].bitcast(U32).indirect(offs_l[:]))
        M_SPLIT = 24
        nc.scalar.copy(
            w_bf[:, :, P // 2 : P // 2 + M_SPLIT, :].rearrange("p t m j -> p m j t"),
            w_raw[1][:, :, : M_SPLIT * PACK].rearrange("p j (m t) -> p m j t", t=PACK),
        )
        nc.vector.tensor_copy(
            w_bf[:, :, P // 2 + M_SPLIT :, :].rearrange("p t m j -> p m j t"),
            w_raw[1][:, :, M_SPLIT * PACK :].rearrange("p j (m t) -> p m j t", t=PACK),
        )
        y_ps = [psum.tile([P, S], F32, name=f"y_ps{t}") for t in range(PACK)]
        for t in range(PACK):
            cols = slice(t * P, (t + 1) * P)
            nc.vector.quantize_mx(
                out=w_codes[:, cols].bitcast(FP8X4), scales=w_sc[:, cols], in_=w_bf[:, t].rearrange("p m j -> p (m j)")
            )
            nc.tensor.matmul_mx(
                out=y_ps[t][:], lhsT=w_codes[:, cols].bitcast(FP8X4), lhsT_scale=w_sc[:, cols],
                rhs=xw[:].bitcast(FP8X4), rhs_scale=xs[:], start=True, stop=True,
            )

        es = sb("es", [P, Z], U8)
        nc.vector.tensor_copy(es[:], es_all[:].indirect(prt_l[:]))

        last = PACK - 1
        ON_GPSIMD = 2
        exu = sb("exu", [P, PACK - ON_GPSIMD, V], F32)
        for t in range(ON_GPSIMD, PACK):
            nc.gpsimd.tensor_scalar(
                exu[:, t - ON_GPSIMD, :], exq_sb[:, t, :], unit_sb[:, t : t + 1], 0.0, ALU.mult, ALU.add
            )

        hid_flat = sb("hid_flat", [P, PACK * V], F32)
        hid = hid_flat[:].rearrange("p (t v) -> p t v", t=PACK)
        rng = [sb(f"rng{t}", [P, S], F32) for t in range(PACK)]
        y1 = [sb(f"y1_{t}", [P, S], F32)[:] for t in range(last)] + [hid_flat[:, ON_GPSIMD * V :]]
        y2 = [sb(f"y2_{t}", [P, S], F32) for t in range(last)] + [rng[1]]
        picked = [sb(f"picked{t}", [P, V], F32)[:] if t != 2 else y_sb[last][:, :V] for t in range(PACK)]
        halves = [(0, S // 2), (S // 2, S)]

        def gather(on_vector, dst, window, lst, a, b):
            src = window[:].indirect(lst[:, a // 16 : b // 16])
            if on_vector:
                nc.vector.tensor_copy(dst[:, a:b], src)
            else:
                nc.scalar.activation(dst[:, a:b], src, ACT.Copy)

        def innovate(t, a, b):
            nc.vector.scalar_tensor_tensor(
                hid[:, t, a:b], picked[t][:, a:b], unit_sb[:, t : t + 1], exu[:, t - ON_GPSIMD, a:b], ALU.mult, ALU.subtract
            )

        def pick(t):
            gather(False, picked[t], rng[t], ps_l, 0, V)
            if t < ON_GPSIMD:
                nc.gpsimd.tensor_tensor(picked[t], picked[t], exq_sb[:, t, :], ALU.subtract)
                nc.gpsimd.tensor_scalar(hid[:, t, :], picked[t], unit_sb[:, t : t + 1], 0.0, ALU.mult, ALU.add)

        for t in range(last):
            nc.scalar.copy(y_sb[t][:, :S], y_ps[t][:])
            gather(False, y1[t], y_sb[t], bm1_l, 0, S)
            for a, b in halves:
                gather(t < last - 1 or a == 0, y2[t], y_sb[t], bm2_l, a, b)
            nc.vector.tensor_tensor(y1[t], y_ps[t][:], y1[t], ALU.min)
            nc.vector.tensor_tensor(y2[t][:], y_ps[t][:], y2[t][:], ALU.max)
            nc.gpsimd.tensor_tensor(rng[t][:], y1[t], y2[t][:], ALU.add)
        ew = keep.tile([P, Z], U32, name="ew", tag="y2", align_bytes=64)
        nc.vector.tensor_copy(ew[:], ew_all[:].bitcast(U32).indirect(prt_l[:]))
        nc.scalar.copy(y_sb[last][:, :S], y_ps[last][:])
        pick(0)
        gather(False, y1[last], y_sb[last], bm1_l, 0, S)
        nc.vector.tensor_tensor(y1[last], y_ps[last][:], y1[last], ALU.min)
        pick(1)
        for a, b in halves:
            gather(False, y2[last], y_sb[last], bm2_l, a, b)
            nc.vector.tensor_tensor(y2[last][:, a:b], y_ps[last][:, a:b], y2[last][:, a:b], ALU.max)
        nc.vector.tensor_tensor(rng[last][:], y1[last], y2[last][:], ALU.add)
        pick(2)
        for h in range(2):
            gather(h == 0, picked[last], rng[last], ps_l, h * P, (h + 1) * P)
        innovate(2, 0, V)
        for h in range(2):
            innovate(last, h * P, (h + 1) * P)

        h_codes = sb("h_codes", [P, V], U32)
        h_sc = sb("h_sc", [P, V], U8)
        sc_ps = [[psum.tile([P, Z // 2], F32, name=f"sc_ps{h}{c}") for c in range(2)] for h in range(2)]
        for h in range(2):
            cols = slice(h * P, (h + 1) * P)
            h_bf = sb(f"h_bf{h}", [P, P, PACK], BF16)
            (nc.vector.tensor_copy if h == 0 else nc.scalar.copy)(
                h_bf[:].rearrange("p (c i) t -> p c t i", i=4),
                hid[:, :, cols].rearrange("p t (c i) -> p c t i", i=4),
            )
            nc.vector.quantize_mx(
                out=h_codes[:, cols].bitcast(FP8X4), scales=h_sc[:, cols], in_=h_bf[:].rearrange("p v t -> p (v t)")
            )
            for c, (a, b) in enumerate(halves):
                nc.tensor.matmul_mx(
                    out=sc_ps[h][c][:], lhsT=h_codes[:, cols].bitcast(FP8X4), lhsT_scale=h_sc[:, cols],
                    rhs=ew[:, a:b].bitcast(FP8X4), rhs_scale=es[:, a:b], start=True, stop=True,
                )

        wg_tile = keep.tile([P, Z], F32, name="wg_tile", tag="hid_flat", align_bytes=64)
        wg = wg_tile[:]
        gather(True, wg, wgt_all, prt_l, 0, Z)
        th = [sb(f"th{h}", [P, Z], F32) for h in range(2)]
        sq = [sb(f"sq{h}", [P, Z], F32) for h in range(2)]
        ex = [sb(f"ex{h}", [P, Z], F32) for h in range(2)]
        pw = [sb(f"pw{h}", [P, Z], F32) for h in range(2)]
        pa = [sb(f"pa{h}", [P, Z + PAD], F32) for h in range(2)]
        ln = [sb(f"ln{h}", [P, Z], F32) for h in range(2)]
        res = [sb(f"res{h}", [P, Z], F32) for h in range(2)]
        st = [sb(f"st{h}", [P, 4], F32) for h in range(2)]
        inv_col = [Z // 2, 0]
        inv = [pa[1][:, c : c + 1] for c in inv_col]
        neg_inv = [pa[1][:, Z + h : Z + h + 1] for h in range(2)]
        signs = sb("signs", [P, 2], F32)
        nc.vector.memset(signs[:, 0:1], 1.0 / Z)
        nc.vector.memset(signs[:, 1:2], -1.0 / Z)
        for h in range(2):
            for c, (a, b) in enumerate(halves):
                nc.scalar.activation(th[h][:, a:b], sc_ps[h][c][:], ACT.Tanh)
                nc.vector.tensor_tensor(sq[h][:, a:b], th[h][:, a:b], th[h][:, a:b], ALU.mult)
        for h in range(2):
            nc.scalar.activation(ex[h][:], sq[h][:], ACT.Exp, scale=-2.0)
            nc.vector.scalar_tensor_tensor(pw[h][:], ex[h][:], 1.0, wg, ALU.mult, ALU.mult, accum_out=st[h][:, 0:1])
            nc.vector.scalar_tensor_tensor(
                st[h][:, 2:4], st[h][:, 0:1].to_broadcast([P, 2]), 0.1 * Z, signs[:], ALU.add, ALU.mult
            )
            nc.vector.reciprocal(pa[1][:, inv_col[h] : Z + h + 1 : Z + h - inv_col[h]], st[h][:, 2:4])
        halves = [slice(0, Z // 2), slice(Z // 2, Z)]
        for c in range(2):
            nc.vector.tensor_copy(pa[0][:, halves[c]], pw[0][:].indirect(anc_l[:, c * 16 : (c + 1) * 16]))
        for h in range(2):
            nc.scalar.activation(ln[h][:], pw[h][:], ACT.Ln, bias=0.2, scale=inv[h])
        for c in range(2):
            nc.scalar.activation(pa[1][:, halves[c]], pw[1][:].indirect(anc_l[:, c * 16 : (c + 1) * 16]), ACT.Copy)
        nc.vector.tensor_tensor(ln[0][:], ln[0][:], wg, ALU.mult)
        nc.vector.tensor_tensor(ln[1][:], ln[1][:], wg, ALU.mult)
        nc.vector.scalar_tensor_tensor(res[0][:], pa[0][:, :Z], neg_inv[0], ln[0][:], ALU.mult, ALU.add)
        nc.sync.dma_start(out[0:P, :], res[0][:])
        for c in range(2):
            nc.vector.scalar_tensor_tensor(
                res[1][:, halves[c]], pa[1][:, halves[c]], neg_inv[1], ln[1][:, halves[c]], ALU.mult, ALU.add
            )
            nc.sync.dma_start(out[P : 2 * P, halves[c]], res[1][:, halves[c]])
